import numpy as np
import ml_dtypes


def mxq(x, axis, fmt="e4m3"):
    dtype, down = {"e4m3": (ml_dtypes.float8_e4m3fn, 7), "e5m2": (ml_dtypes.float8_e5m2, 14)}[fmt]
    v = np.moveaxis(np.asarray(x, np.float32).astype(ml_dtypes.bfloat16).astype(np.float64), axis, -1)
    blocks = v.reshape(v.shape[:-1] + (-1, 32))
    amax = np.abs(blocks).max(-1, keepdims=True)
    byte = np.maximum(np.where(amax > 0, np.frexp(amax)[1] - 1 + 127, 0) - down, 1)
    scale = np.exp2(byte - 127.0)
    codes = (blocks / scale).astype(np.float32).astype(dtype).astype(np.float64)
    return np.moveaxis((codes * scale).reshape(v.shape), -1, axis)


WIDE = False


def mx_kscale(k):
    if not WIDE:
        return np.ones(k)
    levels = np.array([10, -10, 5, -5, 0])
    if k % 512:
        return np.exp2(np.random.permutation(np.resize(levels, k // 32))).repeat(32)
    a = np.empty((k // 512, 16))
    for p in range(k // 512):
        a[p, :8] = np.random.permutation(np.resize(levels, 8))
        for g in range(8):
            far = levels[np.abs(levels - a[p, g]) >= 10]
            a[p, g + 8] = far[np.random.randint(len(far))]
    return np.exp2(a.ravel()).repeat(32)


def f64(x):
    return np.asarray(x).astype(np.float64)


def striped(idx):
    return np.tile(np.asarray(idx).reshape(-1, 16).T, (8, 1)).astype(np.uint16)


def unstriped(offs):
    return offs[:16].T.reshape(-1).astype(np.int64)


E2M1 = np.array([0.0, 0.5, 1.0, 1.5, 2.0, 3.0, 4.0, 6.0, -0.0, -0.5, -1.0, -1.5, -2.0, -3.0, -4.0, -6.0])


def pack_weight(w, fmt):
    k, n = w.shape
    w = f64(np.asarray(w, np.float32).astype(ml_dtypes.bfloat16)).reshape(k // 32, 32, n)
    amax = np.abs(w).max(1)
    if fmt == "e4m3":
        byte = np.frexp(amax)[1] - 1 + 127 - 7
    else:
        mant, ex = np.frexp(amax / 6.0)
        byte = np.where(mant > 0.5, ex, ex - 1) + 127
    byte = np.clip(np.where(amax > 0, byte, 1), 1, 254)
    scaled = (w * np.exp2(127.0 - byte)[:, None, :]).reshape(k, n).astype(np.float32)
    by_word = np.ascontiguousarray(scaled.reshape(k // 512, 128, 4, n).transpose(0, 1, 3, 2))
    if fmt == "e4m3":
        words = by_word.astype(ml_dtypes.float8_e4m3fn).view(np.uint8)
    else:
        c = by_word.astype(ml_dtypes.float4_e2m1fn).view(np.uint8) & 0xF
        words = (c[..., 0::2] | (c[..., 1::2] << 4)).reshape(k // 512, 128, 2 * n)
    return np.ascontiguousarray(words), np.ascontiguousarray(byte.astype(np.uint8).reshape(k // 512, 16, n))


def unpack_weight(words, scales, fmt):
    g, _, n = scales.shape
    words = np.ascontiguousarray(words).reshape(g, 128, n, -1)
    if fmt == "e4m3":
        vals = words.view(ml_dtypes.float8_e4m3fn).astype(np.float64)
    else:
        nib = np.empty((g, 128, n, 4), np.uint8)
        nib[..., 0::2] = words & 0xF
        nib[..., 1::2] = words >> 4
        vals = E2M1[nib]
    vals = vals * np.repeat(np.exp2(scales.astype(np.float64) - 127.0), 8, axis=1)[..., None]
    return vals.transpose(0, 1, 3, 2).reshape(g * 512, n)


K, T, J, N = 1024, 2048, 512, 512


def setup_inputs():
    n = np.random.standard_normal
    idx = np.random.permutation(T)[:J]
    fk = mx_kscale(K)
    xtp = pack_weight(n((K, T)) * np.random.uniform(0.3, 1.7, (1, T)) / fk[:, None], "e4m3")
    wbp = pack_weight(n((K, N)) * np.random.uniform(0.2, 1.6, (K, 1)) / np.sqrt(K) * fk[:, None], "e2m1")
    wcp = pack_weight(n((K, N)) * 0.6 / np.sqrt(K) * fk[:, None], "e4m3")
    return {
        "xt_words": xtp[0],
        "xt_scales": xtp[1],
        "wa": (n((K, N)) * 1 / np.sqrt(K) * fk[:, None]).astype(np.float32),
        "wb_words": wbp[0],
        "wb_scales": wbp[1],
        "wc_words": wcp[0],
        "wc_scales": wcp[1],
        "bi": (np.random.uniform(-0.5, 0.5, (1, N))).astype(np.float32),
        "offs": striped(idx),
    }


def reference(xt_words, xt_scales, wa, wb_words, wb_scales, wc_words, wc_scales, bi, offs):
    idx = unstriped(offs)
    xtu = unpack_weight(xt_words, xt_scales, "e4m3")
    wbu = unpack_weight(wb_words, wb_scales, "e2m1")
    wcu = unpack_weight(wc_words, wc_scales, "e4m3")
    xtidxg = xtu[:, idx]
    waq = mxq(f64(wa), 0, "e4m3")
    a = xtidxg.T @ waq
    b = xtidxg.T @ wbu
    e = xtidxg.T @ wcu
    ea = np.exp(np.mean(np.square(a), axis=1, keepdims=True))
    eb = np.exp(np.mean(np.square(b), axis=1, keepdims=True))
    ec = np.exp(np.mean(np.square(e), axis=1, keepdims=True))
    y = (ea * a + eb * b + ec * e) / (ea + eb + ec) + f64(bi)
    return y

@@ -1,0 +1,214 @@
+from contextlib import ExitStack
+
+import concourse.mybir as mybir
+from concourse.masks import make_identity
+
+K, T, J, N = 1024, 2048, 512, 512
+FLOPS = 3 * 2 * J * K * N
+
+F32 = mybir.dt.float32
+BF16 = mybir.dt.bfloat16
+I32 = mybir.dt.int32
+U32 = mybir.dt.uint32
+U16 = mybir.dt.uint16
+U8 = mybir.dt.uint8
+E4M3X4 = mybir.dt.float8_e4m3fn_x4
+E2M1X4 = mybir.dt.float4_e2m1fn_x4
+ALU = mybir.AluOpType
+ACT = mybir.ActivationFunctionType
+
+P = 128
+PACK = 4
+PASSES = K // (P * PACK)
+BLOCKS = J // P
+QUADS = 4
+ROOT = 1.0 / 32.0
+
+
+def tile_moe_three_experts_by_energy_kernel(
+    tc, xt_words, xt_scales, wa, wb_words, wb_scales, wc_words, wc_scales, bi, offs, out
+):
+    nc = tc.nc
+    with ExitStack() as ctx:
+        keep = ctx.enter_context(tc.tile_pool(name="keep", bufs=1))
+        ring = ctx.enter_context(tc.tile_pool(name="ring", bufs=2))
+        psum = ctx.enter_context(tc.psum_pool(name="psum", bufs=1))
+
+        offsets = keep.tile([P, J // 16], U16, name="offsets")
+        nc.sync.dma_start(offsets[:], offs)
+
+        warm = keep.tile([P, 1], F32, name="warm")
+        warm2 = keep.tile([P, 1], F32, name="warm2")
+        nc.gpsimd.memset(warm[:], 0.0)
+        nc.scalar.activation(warm2[:], warm[:], ACT.Tanh)
+
+        def zeroed(name, width):
+            plane = keep.tile([P, width], U8, name=name, align_bytes=64)
+            nc.vector.memset(plane[:].bitcast(I32), 0)
+            return plane
+
+        x_scale = zeroed("x_scale", PASSES * T)
+        b_scale = zeroed("b_scale", PASSES * N)
+        c_scale = zeroed("c_scale", PASSES * N)
+
+        def load_scales(plane, scales, first):
+            rows = plane[:].bitcast(I32).rearrange("p (z c) -> p z c", z=PASSES)
+            src = scales.bitcast(I32).rearrange("z (q r) c -> r q z c", r=4)
+            for r in range(4):
+                nc.sync.dma_start(rows[first + r : P : 32], src[r])
+
+        x_words = [keep.tile([P, T], U32, name="x_words%d" % z, align_bytes=64) for z in range(PASSES)]
+        b_words = keep.tile([P, PASSES * 2 * N], U8, name="b_words", align_bytes=64)
+        c_words = keep.tile([P, PASSES * N], U32, name="c_words", align_bytes=64)
+
+        def load_x(z):
+            nc.sync.dma_start(x_words[z][:].bitcast(I32), xt_words[z].rearrange("p c r -> p (c r)").bitcast(I32))
+
+        bias_rows = keep.tile([P, PACK], F32, name="bias_rows")
+        nc.gpsimd.dma_start(bias_rows[:], bi.rearrange("o (p c) -> (o p) c", c=PACK))
+
+        half = N // 2
+        pieces = [(0, 0, half), (0, half, N), (1, 0, half), (1, half, N)]
+        raws = []
+
+        def load_wa(n):
+            z, c0, c1 = pieces[n]
+            raw = keep.tile([P, PACK, c1 - c0], F32, name="raw%d" % n, tag="raw%d" % n)
+            nc.sync.dma_start(raw[:], wa[z * P * PACK : (z + 1) * P * PACK, c0:c1].rearrange("(p j) c -> p j c", j=PACK))
+            raws.append(raw)
+
+        load_x(0)
+        load_scales(x_scale, xt_scales, 0)
+        load_x(1)
+        nc.sync.dma_start(
+            b_words[:].bitcast(I32).rearrange("p (z c) -> p z c", z=PASSES),
+            wb_words.bitcast(I32).rearrange("z p c -> p z c"),
+        )
+        load_scales(b_scale, wb_scales, 0)
+        nc.sync.dma_start(
+            c_words[:].bitcast(I32).rearrange("p (z c) -> p z c", z=PASSES),
+            wc_words.rearrange("z p c r -> z p (c r)").bitcast(I32).rearrange("z p c -> p z c"),
+        )
+        load_wa(0)
+        load_scales(c_scale, wc_scales, 8)
+        for n in range(1, len(pieces)):
+            load_wa(n)
+
+        g0 = keep.tile([P, J], U32, name="g_words0", align_bytes=64)
+        nc.vector.tensor_copy(g0[:], x_words[0][:].indirect(offsets[:]))
+        g_scale = [keep.tile([P, J], U8, name="g_scale%d" % z, align_bytes=64) for z in range(PASSES)]
+        for z in range(PASSES):
+            nc.vector.tensor_copy(g_scale[z][:], x_scale[:, z * T : (z + 1) * T].indirect(offsets[:]))
+        g1 = [keep.tile([P, J // 2], U32, name="g_words1_%d" % h, align_bytes=64) for h in range(2)]
+        for h in range(2):
+            nc.vector.tensor_copy(g1[h][:], x_words[1][:].indirect(offsets[:, h * 16 : (h + 1) * 16]))
+
+        ident = keep.tile([P, P], F32, name="ident")
+        make_identity(nc, ident[:])
+        spread = psum.tile([P, PACK, P], F32, name="spread", tag="bank7")
+        for c in range(PACK):
+            nc.tensor.transpose(spread[:, c, :], bias_rows[:, c : c + 1].to_broadcast([P, P]), ident[:])
+        bias = keep.tile([P, N], F32, name="bias")
+        nc.scalar.copy(bias[:].rearrange("p (q c) -> p q c", c=PACK), spread[:].rearrange("p c q -> p q c"))
+
+        def tokens(z, j):
+            if z == 0:
+                return g0[:, j * P : (j + 1) * P]
+            return g1[j // 2][:, (j % 2) * P : (j % 2 + 1) * P]
+
+        def product(acc, j, z, words, scale):
+            nc.tensor.matmul_mx(
+                out=acc[:],
+                lhsT=tokens(z, j).bitcast(E4M3X4),
+                lhsT_scale=g_scale[z][:, j * P : (j + 1) * P],
+                rhs=words,
+                rhs_scale=scale,
+                start=(z == 0),
+                stop=(z == PASSES - 1),
+            )
+
+        acc_b = [psum.tile([P, N], F32, name="acc_b%d" % j, tag="bank%d" % j) for j in range(BLOCKS)]
+        acc_c = [psum.tile([P, N], F32, name="acc_c%d" % j, tag="bank%d" % (BLOCKS + j)) for j in range(BLOCKS)]
+        for j in range(BLOCKS):
+            for z in range(PASSES):
+                product(acc_b[j], j, z, b_words[:, z * 2 * N : (z + 1) * 2 * N].bitcast(E2M1X4), b_scale[:, z * N : (z + 1) * N])
+        for j in range(BLOCKS):
+            for z in range(PASSES):
+                product(acc_c[j], j, z, c_words[:, z * N : (z + 1) * N].bitcast(E4M3X4), c_scale[8:P, z * N : (z + 1) * N])
+
+        def energy(acc, name):
+            h = keep.tile([P, 1], F32, name=name)
+            junk = ring.tile([P, N], BF16, name="junk")
+            nc.scalar.activation(junk[:], acc[:], ACT.Square, scale=ROOT, accum_out=h[:])
+            return h
+
+        def small(name):
+            return keep.tile([P, 1], F32, name=name)
+
+        a_words = [keep.tile([P, N], U32, name="a_words%d" % z, align_bytes=64) for z in range(PASSES)]
+        a_scale = [keep.tile([P, N], U8, name="a_scale%d" % z, align_bytes=64) for z in range(PASSES)]
+
+        def quantise(raw, r0, z, c0, width):
+            grouped = ring.tile([P, width * PACK], BF16, name="grouped", align_bytes=64)
+            nc.vector.tensor_copy(
+                grouped[:].rearrange("p (c i t) -> p c t i", i=4, t=PACK),
+                raw[:, :, r0 : r0 + width].rearrange("p t (c i) -> p c t i", i=4),
+            )
+            nc.vector.quantize_mx(
+                out=a_words[z][:, c0 : c0 + width].bitcast(E4M3X4), scales=a_scale[z][:, c0 : c0 + width], in_=grouped[:]
+            )
+
+        for raw, (z, c0, c1) in zip(raws, pieces):
+            quantise(raw, 0, z, c0, half)
+        h_b = [energy(acc_b[j], "hb%d" % j) for j in range(BLOCKS)]
+        late = keep.tile([P, BLOCKS, N], F32, name="late", tag="raw3")
+        pair, top, slope, base = [], [], [], []
+        for j in range(BLOCKS):
+            hb = h_b[j]
+            hc = energy(acc_c[j], "hc%d" % j)
+            t0 = small("t0_%d" % j)
+            nc.scalar.activation(t0[:], hc[:], ACT.Tanh, bias=hb[:], scale=-1.0)
+            kc = small("kc%d" % j)
+            nc.scalar.activation(kc[:], t0[:], ACT.Copy, bias=1.0, scale=-1.0)
+            kb = small("kb%d" % j)
+            nc.scalar.activation(kb[:], t0[:], ACT.Copy, bias=1.0, scale=1.0)
+            part = keep.tile([P, N], F32, name="part%d" % j)
+            nc.scalar.activation(part[:], acc_c[j][:], ACT.Copy, scale=kc[:])
+            u = late[:, j, :]
+            nc.vector.scalar_tensor_tensor(u, acc_b[j][:], kb[:], part[:], ALU.mult, ALU.add)
+            h = small("top%d" % j)
+            nc.gpsimd.tensor_scalar(h[:], hb[:], hc[:], None, ALU.max)
+            p = small("slope%d" % j)
+            nc.gpsimd.tensor_scalar(p[:], kb[:], kc[:], None, ALU.min)
+            q = small("base%d" % j)
+            nc.gpsimd.tensor_scalar(q[:], p[:], -1.0, 4.0, ALU.mult, ALU.add)
+            pair.append(u)
+            top.append(h)
+            slope.append(p)
+            base.append(q)
+
+        def shares(j):
+            acc_a = psum.tile([P, N], F32, name="acc_a%d" % j, tag="bank%d" % (BLOCKS + j))
+            for z in range(PASSES):
+                product(acc_a, j, z, a_words[z][:].bitcast(E4M3X4), a_scale[z][:])
+            squares = keep.tile([P, N + 8], F32, name="squares")
+            nc.scalar.activation(squares[:, 0:N], acc_a[:], ACT.Square, scale=ROOT, accum_out=squares[:, N : N + 1])
+            t1 = small("t1_%d" % j)
+            nc.scalar.activation(t1[:], squares[:, N : N + 1], ACT.Tanh, bias=top[j][:], scale=-1.0)
+            den = small("den%d" % j)
+            nc.vector.tensor_scalar(den[:], t1[:], slope[j][:], base[j][:], ALU.mult, ALU.add)
+            inv = small("inv%d" % j)
+            nc.vector.reciprocal(inv[:], den[:])
+            mu = small("mu%d" % j)
+            nc.vector.tensor_scalar(mu[:], t1[:], 1.0, inv[:], ALU.add, ALU.mult)
+            alpha = small("alpha%d" % j)
+            nc.vector.tensor_scalar(alpha[:], mu[:], -2.0, 1.0, ALU.mult, ALU.add)
+            return acc_a, mu, alpha
+
+        mixes = [shares(j) for j in range(BLOCKS)]
+        for j, (acc_a, mu, alpha) in enumerate(mixes):
+            rest = ring.tile([P, N], F32, name="rest")
+            nc.vector.scalar_tensor_tensor(rest[:], pair[j], mu[:], bias[:], ALU.mult, ALU.add)
+            res = keep.tile([P, N], F32, name="res%d" % j)
+            nc.vector.scalar_tensor_tensor(res[:], acc_a[:], alpha[:], rest[:], ALU.mult, ALU.add)
+            nc.sync.dma_start(out[j * P : (j + 1) * P, :], res[:])

@@ -23,6 +23,7 @@ PASSES = K // (P * PACK)
 BLOCKS = J // P
 QUADS = 4
 ROOT = 1.0 / 32.0
+EARLY = 2
 
 
 def tile_moe_three_experts_by_energy_kernel(
@@ -35,12 +36,15 @@ def tile_moe_three_experts_by_energy_kernel(
         psum = ctx.enter_context(tc.psum_pool(name="psum", bufs=1))
 
         offsets = keep.tile([P, J // 16], U16, name="offsets")
-        nc.sync.dma_start(offsets[:], offs)
 
-        warm = keep.tile([P, 1], F32, name="warm")
-        warm2 = keep.tile([P, 1], F32, name="warm2")
-        nc.gpsimd.memset(warm[:], 0.0)
-        nc.scalar.activation(warm2[:], warm[:], ACT.Tanh)
+        signs = keep.tile([P, 2], F32, name="signs")
+        nc.gpsimd.memset(signs[:, 0:1], 1.0)
+        nc.gpsimd.memset(signs[:, 1:2], -1.0)
+        lift = keep.tile([P, 2], F32, name="lift")
+        nc.gpsimd.memset(lift[:, 0:1], 2.0)
+        nc.gpsimd.memset(lift[:, 1:2], 0.0)
+        warm = keep.tile([P, 2], F32, name="warm")
+        nc.scalar.activation(warm[:], signs[:], ACT.Exp)
 
         def zeroed(name, width):
             plane = keep.tile([P, width], U8, name=name, align_bytes=64)
@@ -78,6 +82,7 @@ def tile_moe_three_experts_by_energy_kernel(
             raws.append(raw)
 
         load_x(0)
+        nc.sync.dma_start(offsets[:], offs)
         load_scales(x_scale, xt_scales, 0)
         load_x(1)
         nc.sync.dma_start(
@@ -116,31 +121,45 @@ def tile_moe_three_experts_by_energy_kernel(
                 return g0[:, j * P : (j + 1) * P]
             return g1[j // 2][:, (j % 2) * P : (j % 2 + 1) * P]
 
-        def product(acc, j, z, words, scale):
+        def product(acc, j, z, words, scale, n):
             nc.tensor.matmul_mx(
                 out=acc[:],
                 lhsT=tokens(z, j).bitcast(E4M3X4),
                 lhsT_scale=g_scale[z][:, j * P : (j + 1) * P],
                 rhs=words,
                 rhs_scale=scale,
-                start=(z == 0),
-                stop=(z == PASSES - 1),
+                start=(n == 0),
+                stop=(n == PASSES - 1),
+            )
+
+        idle = psum.tile([P, N], F32, name="idle", tag="bank6")
+        for n in range(3):
+            nc.tensor.matmul_mx(
+                out=idle[:],
+                lhsT=g0[:, 0:P].bitcast(E4M3X4),
+                lhsT_scale=g_scale[0][:, 0:P],
+                rhs=g0[:].bitcast(E4M3X4),
+                rhs_scale=g_scale[0][:],
+                start=True,
+                stop=True,
             )
 
         acc_b = [psum.tile([P, N], F32, name="acc_b%d" % j, tag="bank%d" % j) for j in range(BLOCKS)]
-        acc_c = [psum.tile([P, N], F32, name="acc_c%d" % j, tag="bank%d" % (BLOCKS + j)) for j in range(BLOCKS)]
+        acc_c = [psum.tile([P, N], F32, name="acc_c%d" % j, tag="bank%d" % (BLOCKS + j)) for j in range(EARLY)]
         for j in range(BLOCKS):
             for z in range(PASSES):
-                product(acc_b[j], j, z, b_words[:, z * 2 * N : (z + 1) * 2 * N].bitcast(E2M1X4), b_scale[:, z * N : (z + 1) * N])
-        for j in range(BLOCKS):
-            for z in range(PASSES):
-                product(acc_c[j], j, z, c_words[:, z * N : (z + 1) * N].bitcast(E4M3X4), c_scale[8:P, z * N : (z + 1) * N])
+                product(acc_b[j], j, z, b_words[:, z * 2 * N : (z + 1) * 2 * N].bitcast(E2M1X4), b_scale[:, z * N : (z + 1) * N], z)
 
-        def energy(acc, name):
-            h = keep.tile([P, 1], F32, name=name)
+        def third(j):
+            for z in range(PASSES):
+                product(acc_c[j], j, z, c_words[:, z * N : (z + 1) * N].bitcast(E4M3X4), c_scale[8:P, z * N : (z + 1) * N], z)
+
+        for j in range(EARLY):
+            third(j)
+
+        def energy(acc, h):
             junk = ring.tile([P, N], BF16, name="junk")
-            nc.scalar.activation(junk[:], acc[:], ACT.Square, scale=ROOT, accum_out=h[:])
-            return h
+            nc.scalar.activation(junk[:], acc[:], ACT.Square, scale=ROOT, accum_out=h)
 
         def small(name):
             return keep.tile([P, 1], F32, name=name)
@@ -149,7 +168,7 @@ def tile_moe_three_experts_by_energy_kernel(
         a_scale = [keep.tile([P, N], U8, name="a_scale%d" % z, align_bytes=64) for z in range(PASSES)]
 
         def quantise(raw, r0, z, c0, width):
-            grouped = ring.tile([P, width * PACK], BF16, name="grouped", align_bytes=64)
+            grouped = keep.tile([P, width * PACK], BF16, name="grouped%d_%d" % (z, c0), tag="grouped%d_%d" % (z, c0), align_bytes=64)
             nc.vector.tensor_copy(
                 grouped[:].rearrange("p (c i t) -> p c t i", i=4, t=PACK),
                 raw[:, :, r0 : r0 + width].rearrange("p t (c i) -> p c t i", i=4),
@@ -160,55 +179,124 @@ def tile_moe_three_experts_by_energy_kernel(
 
         for raw, (z, c0, c1) in zip(raws, pieces):
             quantise(raw, 0, z, c0, half)
-        h_b = [energy(acc_b[j], "hb%d" % j) for j in range(BLOCKS)]
-        late = keep.tile([P, BLOCKS, N], F32, name="late", tag="raw3")
-        pair, top, slope, base = [], [], [], []
+        h_b = [keep.tile([P, 3], F32, name="h%d" % j) for j in range(BLOCKS)]
         for j in range(BLOCKS):
-            hb = h_b[j]
-            hc = energy(acc_c[j], "hc%d" % j)
-            t0 = small("t0_%d" % j)
-            nc.scalar.activation(t0[:], hc[:], ACT.Tanh, bias=hb[:], scale=-1.0)
-            kc = small("kc%d" % j)
-            nc.scalar.activation(kc[:], t0[:], ACT.Copy, bias=1.0, scale=-1.0)
-            kb = small("kb%d" % j)
-            nc.scalar.activation(kb[:], t0[:], ACT.Copy, bias=1.0, scale=1.0)
-            part = keep.tile([P, N], F32, name="part%d" % j)
-            nc.scalar.activation(part[:], acc_c[j][:], ACT.Copy, scale=kc[:])
-            u = late[:, j, :]
-            nc.vector.scalar_tensor_tensor(u, acc_b[j][:], kb[:], part[:], ALU.mult, ALU.add)
-            h = small("top%d" % j)
-            nc.gpsimd.tensor_scalar(h[:], hb[:], hc[:], None, ALU.max)
-            p = small("slope%d" % j)
-            nc.gpsimd.tensor_scalar(p[:], kb[:], kc[:], None, ALU.min)
-            q = small("base%d" % j)
-            nc.gpsimd.tensor_scalar(q[:], p[:], -1.0, 4.0, ALU.mult, ALU.add)
-            pair.append(u)
-            top.append(h)
-            slope.append(p)
-            base.append(q)
+            energy(acc_b[j], h_b[j][:, 0:1])
+        late = keep.tile([P, EARLY, N], F32, name="late", tag="grouped1_%d" % half, align_bytes=64)
+        top, coef = [], []
 
-        def shares(j):
-            acc_a = psum.tile([P, N], F32, name="acc_a%d" % j, tag="bank%d" % (BLOCKS + j))
-            for z in range(PASSES):
-                product(acc_a, j, z, a_words[z][:].bitcast(E4M3X4), a_scale[z][:])
+        def pair(j):
+            hb = h_b[j][:, 0:1]
+            hc = h_b[j][:, 1:2]
+            energy(acc_c[j], hc)
+            t0 = small("t0_%d" % j)
+            nc.scalar.activation(t0[:], hc, ACT.Tanh, bias=hb, scale=-1.0)
+            k = keep.tile([P, 2], F32, name="k%d" % j)
+            nc.scalar.activation(k[:], signs[:], ACT.Copy, bias=1.0, scale=t0[:])
+            kb, kc = k[:, 0:1], k[:, 1:2]
+            if j == 0:
+                part = keep.tile([P, N], F32, name="part%d" % j)[:]
+                nc.scalar.activation(part, acc_c[j][:], ACT.Copy, scale=kc)
+            else:
+                part = late[:, j, :]
+                nc.vector.tensor_scalar(part, acc_c[j][:], kc, None, ALU.mult)
+            nc.vector.scalar_tensor_tensor(late[:, j, :], acc_b[j][:], kb, part, ALU.mult, ALU.add)
+            h = small("top%d" % j)
+            nc.gpsimd.tensor_scalar(h[:], hb, hc, None, ALU.max)
+            line = keep.tile([P, 2, 3], F32, name="line%d" % j)
+            nc.gpsimd.memset(line[:, :, 0:1], 1.0)
+            nc.gpsimd.tensor_scalar(line[:, 0, 2:3], kb, kc, -1.0, ALU.max, ALU.mult)
+            nc.gpsimd.tensor_scalar(line[:, 0, 1:2], kb, kc, None, ALU.min)
+            nc.gpsimd.tensor_scalar(line[:, 1, 1:3], lift[:], line[:, 0, 2:3], None, ALU.subtract)
+            top.append(h)
+            coef.append(line)
+
+        def first(j, order):
+            bank = BLOCKS + (j + EARLY) % BLOCKS
+            acc_a = psum.tile([P, N], F32, name="acc_a%d" % j, tag="bank%d" % bank)
+            for n, z in enumerate(order):
+                product(acc_a, j, z, a_words[z][:].bitcast(E4M3X4), a_scale[z][:], n)
+            return acc_a
+
+        def early_shares(j):
+            acc_a = first(j, (0, 1))
             squares = keep.tile([P, N + 8], F32, name="squares")
             nc.scalar.activation(squares[:, 0:N], acc_a[:], ACT.Square, scale=ROOT, accum_out=squares[:, N : N + 1])
             t1 = small("t1_%d" % j)
             nc.scalar.activation(t1[:], squares[:, N : N + 1], ACT.Tanh, bias=top[j][:], scale=-1.0)
-            den = small("den%d" % j)
-            nc.vector.tensor_scalar(den[:], t1[:], slope[j][:], base[j][:], ALU.mult, ALU.add)
+            terms = keep.tile([P, 3], F32, name="terms%d" % j)
             inv = small("inv%d" % j)
-            nc.vector.reciprocal(inv[:], den[:])
-            mu = small("mu%d" % j)
-            nc.vector.tensor_scalar(mu[:], t1[:], 1.0, inv[:], ALU.add, ALU.mult)
-            alpha = small("alpha%d" % j)
-            nc.vector.tensor_scalar(alpha[:], mu[:], -2.0, 1.0, ALU.mult, ALU.add)
-            return acc_a, mu, alpha
+            w = keep.tile([P, 3], F32, name="w%d" % j)
+            steps = [
+                lambda: nc.vector.scalar_tensor_tensor(
+                    terms[:], coef[j][:, 0, :], t1[:], coef[j][:, 1, :], ALU.mult, ALU.add
+                ),
+                lambda: nc.vector.reciprocal(inv[:], terms[:, 1:2]),
+                lambda: nc.vector.tensor_scalar(w[:], terms[:], inv[:], None, ALU.mult),
+            ]
+            return acc_a, w, steps
 
-        mixes = [shares(j) for j in range(BLOCKS)]
-        for j, (acc_a, mu, alpha) in enumerate(mixes):
-            rest = ring.tile([P, N], F32, name="rest")
-            nc.vector.scalar_tensor_tensor(rest[:], pair[j], mu[:], bias[:], ALU.mult, ALU.add)
-            res = keep.tile([P, N], F32, name="res%d" % j)
-            nc.vector.scalar_tensor_tensor(res[:], acc_a[:], alpha[:], rest[:], ALU.mult, ALU.add)
-            nc.sync.dma_start(out[j * P : (j + 1) * P, :], res[:])
+        def late_shares(j):
+            acc_c.append(psum.tile([P, N], F32, name="acc_c%d" % j, tag="bank%d" % (j - EARLY)))
+            third(j)
+            acc_a = first(j, (1, 0))
+            h = h_b[j]
+            for acc, col in ((acc_c[j], 1), (acc_a, 2)):
+                squares = keep.tile([P, N + 8], F32, name="squares")
+                nc.scalar.activation(squares[:, 0:N], acc[:], ACT.Square, scale=ROOT, accum_out=h[:, col : col + 1])
+            lowered = keep.tile([P, 3], F32, name="lowered%d" % j)
+            low = small("low%d" % j)
+            grown = keep.tile([P, 3], F32, name="grown%d" % j)
+            summed = small("summed%d" % j)
+            inv = small("inv%d" % j)
+            w = keep.tile([P, 3], F32, name="w%d" % j)
+
+            def exps():
+                nc.vector.tensor_scalar(lowered[:], h[:], -2.0, None, ALU.mult, ALU.min, accum_out=low[:])
+                nc.scalar.activation(grown[:], h[:], ACT.Exp, bias=low[:], scale=2.0, accum_out=summed[:])
+
+            steps = [
+                exps,
+                lambda: nc.vector.reciprocal(inv[:], summed[:]),
+                lambda: nc.vector.tensor_scalar(w[:], grown[:], inv[:], None, ALU.mult),
+            ]
+            return acc_a, w, steps
+
+        def mix_steps(j, acc_a, w):
+            total = keep.tile([P, N], F32, name="total%d" % j)
+            if j < EARLY:
+                addends = [(late[:, j, :], 0), (acc_a[:], 2)]
+            else:
+                addends = [(acc_b[j][:], 0), (acc_c[j][:], 1), (acc_a[:], 2)]
+            steps = []
+            for n, (x, col) in enumerate(addends):
+                for c0 in (0, half):
+                    cols = slice(c0, c0 + half)
+                    prior = bias if n == 0 else total
+                    steps.append(
+                        lambda x=x, col=col, cols=cols, prior=prior: nc.vector.scalar_tensor_tensor(
+                            total[:, cols], x[:, cols], w[:, col : col + 1], prior[:, cols], ALU.mult, ALU.add
+                        )
+                    )
+            return total, steps
+
+        for j in range(EARLY):
+            pair(j)
+        acc_a, w, steps = early_shares(0)
+        for step in steps:
+            step()
+        for j in range(BLOCKS):
+            total, wide = mix_steps(j, acc_a, w)
+            narrow = []
+            if j + 1 < BLOCKS:
+                acc_a, w, narrow = early_shares(j + 1) if j + 1 < EARLY else late_shares(j + 1)
+            lead = len(wide) - 1 - len(narrow)
+            for n, step in enumerate(wide):
+                step()
+                if lead <= n < lead + len(narrow):
+                    narrow[n - lead]()
+                if j + 1 == BLOCKS and n >= len(wide) - 2:
+                    c0 = (n - len(wide) + 2) * half
+                    nc.sync.dma_start(out[j * P : (j + 1) * P, c0 : c0 + half], total[:, c0 : c0 + half])
+            if j + 1 < BLOCKS:
+                nc.sync.dma_start(out[j * P : (j + 1) * P, :], total[:])

@@ -43,8 +43,6 @@ def tile_moe_three_experts_by_energy_kernel(
         lift = keep.tile([P, 2], F32, name="lift")
         nc.gpsimd.memset(lift[:, 0:1], 2.0)
         nc.gpsimd.memset(lift[:, 1:2], 0.0)
-        warm = keep.tile([P, 2], F32, name="warm")
-        nc.scalar.activation(warm[:], signs[:], ACT.Exp)
 
         def zeroed(name, width):
             plane = keep.tile([P, width], U8, name=name, align_bytes=64)
@@ -130,18 +128,6 @@ def tile_moe_three_experts_by_energy_kernel(
                 rhs_scale=scale,
                 start=(n == 0),
                 stop=(n == PASSES - 1),
-            )
-
-        idle = psum.tile([P, N], F32, name="idle", tag="bank6")
-        for n in range(3):
-            nc.tensor.matmul_mx(
-                out=idle[:],
-                lhsT=g0[:, 0:P].bitcast(E4M3X4),
-                lhsT_scale=g_scale[0][:, 0:P],
-                rhs=g0[:].bitcast(E4M3X4),
-                rhs_scale=g_scale[0][:],
-                start=True,
-                stop=True,
             )
 
         acc_b = [psum.tile([P, N], F32, name="acc_b%d" % j, tag="bank%d" % j) for j in range(BLOCKS)]

from contextlib import ExitStack

import concourse.mybir as mybir
from concourse.masks import make_identity

K, T, J, N = 1024, 2048, 512, 512
FLOPS = 3 * 2 * J * K * N

F32 = mybir.dt.float32
BF16 = mybir.dt.bfloat16
I32 = mybir.dt.int32
U32 = mybir.dt.uint32
U16 = mybir.dt.uint16
U8 = mybir.dt.uint8
E4M3X4 = mybir.dt.float8_e4m3fn_x4
E2M1X4 = mybir.dt.float4_e2m1fn_x4
ALU = mybir.AluOpType
ACT = mybir.ActivationFunctionType

P = 128
PACK = 4
PASSES = K // (P * PACK)
BLOCKS = J // P
QUADS = 4
ROOT = 1.0 / 32.0
EARLY = 2


def tile_moe_three_experts_by_energy_kernel(
    tc, xt_words, xt_scales, wa, wb_words, wb_scales, wc_words, wc_scales, bi, offs, out
):
    nc = tc.nc
    with ExitStack() as ctx:
        keep = ctx.enter_context(tc.tile_pool(name="keep", bufs=1))
        ring = ctx.enter_context(tc.tile_pool(name="ring", bufs=2))
        psum = ctx.enter_context(tc.psum_pool(name="psum", bufs=1))

        offsets = keep.tile([P, J // 16], U16, name="offsets")

        signs = keep.tile([P, 2], F32, name="signs")
        nc.gpsimd.memset(signs[:, 0:1], 1.0)
        nc.gpsimd.memset(signs[:, 1:2], -1.0)
        lift = keep.tile([P, 2], F32, name="lift")
        nc.gpsimd.memset(lift[:, 0:1], 2.0)
        nc.gpsimd.memset(lift[:, 1:2], 0.0)

        def zeroed(name, width):
            plane = keep.tile([P, width], U8, name=name, align_bytes=64)
            nc.vector.memset(plane[:].bitcast(I32), 0)
            return plane

        x_scale = zeroed("x_scale", PASSES * T)
        b_scale = zeroed("b_scale", PASSES * N)
        c_scale = zeroed("c_scale", PASSES * N)

        def load_scales(plane, scales, first):
            rows = plane[:].bitcast(I32).rearrange("p (z c) -> p z c", z=PASSES)
            src = scales.bitcast(I32).rearrange("z (q r) c -> r q z c", r=4)
            for r in range(4):
                nc.sync.dma_start(rows[first + r : P : 32], src[r])

        x_words = [keep.tile([P, T], U32, name="x_words%d" % z, align_bytes=64) for z in range(PASSES)]
        b_words = keep.tile([P, PASSES * 2 * N], U8, name="b_words", align_bytes=64)
        c_words = keep.tile([P, PASSES * N], U32, name="c_words", align_bytes=64)

        def load_x(z):
            nc.sync.dma_start(x_words[z][:].bitcast(I32), xt_words[z].rearrange("p c r -> p (c r)").bitcast(I32))

        bias_rows = keep.tile([P, PACK], F32, name="bias_rows")
        nc.gpsimd.dma_start(bias_rows[:], bi.rearrange("o (p c) -> (o p) c", c=PACK))

        half = N // 2
        pieces = [(0, 0, half), (0, half, N), (1, 0, half), (1, half, N)]
        raws = []

        def load_wa(n):
            z, c0, c1 = pieces[n]
            raw = keep.tile([P, PACK, c1 - c0], F32, name="raw%d" % n, tag="raw%d" % n)
            nc.sync.dma_start(raw[:], wa[z * P * PACK : (z + 1) * P * PACK, c0:c1].rearrange("(p j) c -> p j c", j=PACK))
            raws.append(raw)

        load_x(0)
        nc.sync.dma_start(offsets[:], offs)
        load_scales(x_scale, xt_scales, 0)
        load_x(1)
        nc.sync.dma_start(
            b_words[:].bitcast(I32).rearrange("p (z c) -> p z c", z=PASSES),
            wb_words.bitcast(I32).rearrange("z p c -> p z c"),
        )
        load_scales(b_scale, wb_scales, 0)
        nc.sync.dma_start(
            c_words[:].bitcast(I32).rearrange("p (z c) -> p z c", z=PASSES),
            wc_words.rearrange("z p c r -> z p (c r)").bitcast(I32).rearrange("z p c -> p z c"),
        )
        load_wa(0)
        load_scales(c_scale, wc_scales, 8)
        for n in range(1, len(pieces)):
            load_wa(n)

        g0 = keep.tile([P, J], U32, name="g_words0", align_bytes=64)
        nc.vector.tensor_copy(g0[:], x_words[0][:].indirect(offsets[:]))
        g_scale = [keep.tile([P, J], U8, name="g_scale%d" % z, align_bytes=64) for z in range(PASSES)]
        for z in range(PASSES):
            nc.vector.tensor_copy(g_scale[z][:], x_scale[:, z * T : (z + 1) * T].indirect(offsets[:]))
        g1 = [keep.tile([P, J // 2], U32, name="g_words1_%d" % h, align_bytes=64) for h in range(2)]
        for h in range(2):
            nc.vector.tensor_copy(g1[h][:], x_words[1][:].indirect(offsets[:, h * 16 : (h + 1) * 16]))

        ident = keep.tile([P, P], F32, name="ident")
        make_identity(nc, ident[:])
        spread = psum.tile([P, PACK, P], F32, name="spread", tag="bank7")
        for c in range(PACK):
            nc.tensor.transpose(spread[:, c, :], bias_rows[:, c : c + 1].to_broadcast([P, P]), ident[:])
        bias = keep.tile([P, N], F32, name="bias")
        nc.scalar.copy(bias[:].rearrange("p (q c) -> p q c", c=PACK), spread[:].rearrange("p c q -> p q c"))

        def tokens(z, j):
            if z == 0:
                return g0[:, j * P : (j + 1) * P]
            return g1[j // 2][:, (j % 2) * P : (j % 2 + 1) * P]

        def product(acc, j, z, words, scale, n):
            nc.tensor.matmul_mx(
                out=acc[:],
                lhsT=tokens(z, j).bitcast(E4M3X4),
                lhsT_scale=g_scale[z][:, j * P : (j + 1) * P],
                rhs=words,
                rhs_scale=scale,
                start=(n == 0),
                stop=(n == PASSES - 1),
            )

        acc_b = [psum.tile([P, N], F32, name="acc_b%d" % j, tag="bank%d" % j) for j in range(BLOCKS)]
        acc_c = [psum.tile([P, N], F32, name="acc_c%d" % j, tag="bank%d" % (BLOCKS + j)) for j in range(EARLY)]
        for j in range(BLOCKS):
            for z in range(PASSES):
                product(acc_b[j], j, z, b_words[:, z * 2 * N : (z + 1) * 2 * N].bitcast(E2M1X4), b_scale[:, z * N : (z + 1) * N], z)

        def third(j):
            for z in range(PASSES):
                product(acc_c[j], j, z, c_words[:, z * N : (z + 1) * N].bitcast(E4M3X4), c_scale[8:P, z * N : (z + 1) * N], z)

        for j in range(EARLY):
            third(j)

        def energy(acc, h):
            junk = ring.tile([P, N], BF16, name="junk")
            nc.scalar.activation(junk[:], acc[:], ACT.Square, scale=ROOT, accum_out=h)

        def small(name):
            return keep.tile([P, 1], F32, name=name)

        a_words = [keep.tile([P, N], U32, name="a_words%d" % z, align_bytes=64) for z in range(PASSES)]
        a_scale = [keep.tile([P, N], U8, name="a_scale%d" % z, align_bytes=64) for z in range(PASSES)]

        def quantise(raw, r0, z, c0, width):
            grouped = keep.tile([P, width * PACK], BF16, name="grouped%d_%d" % (z, c0), tag="grouped%d_%d" % (z, c0), align_bytes=64)
            nc.vector.tensor_copy(
                grouped[:].rearrange("p (c i t) -> p c t i", i=4, t=PACK),
                raw[:, :, r0 : r0 + width].rearrange("p t (c i) -> p c t i", i=4),
            )
            nc.vector.quantize_mx(
                out=a_words[z][:, c0 : c0 + width].bitcast(E4M3X4), scales=a_scale[z][:, c0 : c0 + width], in_=grouped[:]
            )

        for raw, (z, c0, c1) in zip(raws, pieces):
            quantise(raw, 0, z, c0, half)
        h_b = [keep.tile([P, 3], F32, name="h%d" % j) for j in range(BLOCKS)]
        for j in range(BLOCKS):
            energy(acc_b[j], h_b[j][:, 0:1])
        late = keep.tile([P, EARLY, N], F32, name="late", tag="grouped1_%d" % half, align_bytes=64)
        top, coef = [], []

        def pair(j):
            hb = h_b[j][:, 0:1]
            hc = h_b[j][:, 1:2]
            energy(acc_c[j], hc)
            t0 = small("t0_%d" % j)
            nc.scalar.activation(t0[:], hc, ACT.Tanh, bias=hb, scale=-1.0)
            k = keep.tile([P, 2], F32, name="k%d" % j)
            nc.scalar.activation(k[:], signs[:], ACT.Copy, bias=1.0, scale=t0[:])
            kb, kc = k[:, 0:1], k[:, 1:2]
            if j == 0:
                part = keep.tile([P, N], F32, name="part%d" % j)[:]
                nc.scalar.activation(part, acc_c[j][:], ACT.Copy, scale=kc)
            else:
                part = late[:, j, :]
                nc.vector.tensor_scalar(part, acc_c[j][:], kc, None, ALU.mult)
            nc.vector.scalar_tensor_tensor(late[:, j, :], acc_b[j][:], kb, part, ALU.mult, ALU.add)
            h = small("top%d" % j)
            nc.gpsimd.tensor_scalar(h[:], hb, hc, None, ALU.max)
            line = keep.tile([P, 2, 3], F32, name="line%d" % j)
            nc.gpsimd.memset(line[:, :, 0:1], 1.0)
            nc.gpsimd.tensor_scalar(line[:, 0, 2:3], kb, kc, -1.0, ALU.max, ALU.mult)
            nc.gpsimd.tensor_scalar(line[:, 0, 1:2], kb, kc, None, ALU.min)
            nc.gpsimd.tensor_scalar(line[:, 1, 1:3], lift[:], line[:, 0, 2:3], None, ALU.subtract)
            top.append(h)
            coef.append(line)

        def first(j, order):
            bank = BLOCKS + (j + EARLY) % BLOCKS
            acc_a = psum.tile([P, N], F32, name="acc_a%d" % j, tag="bank%d" % bank)
            for n, z in enumerate(order):
                product(acc_a, j, z, a_words[z][:].bitcast(E4M3X4), a_scale[z][:], n)
            return acc_a

        def early_shares(j):
            acc_a = first(j, (0, 1))
            squares = keep.tile([P, N + 8], F32, name="squares")
            nc.scalar.activation(squares[:, 0:N], acc_a[:], ACT.Square, scale=ROOT, accum_out=squares[:, N : N + 1])
            t1 = small("t1_%d" % j)
            nc.scalar.activation(t1[:], squares[:, N : N + 1], ACT.Tanh, bias=top[j][:], scale=-1.0)
            terms = keep.tile([P, 3], F32, name="terms%d" % j)
            inv = small("inv%d" % j)
            w = keep.tile([P, 3], F32, name="w%d" % j)
            steps = [
                lambda: nc.vector.scalar_tensor_tensor(
                    terms[:], coef[j][:, 0, :], t1[:], coef[j][:, 1, :], ALU.mult, ALU.add
                ),
                lambda: nc.vector.reciprocal(inv[:], terms[:, 1:2]),
                lambda: nc.vector.tensor_scalar(w[:], terms[:], inv[:], None, ALU.mult),
            ]
            return acc_a, w, steps

        def late_shares(j):
            acc_c.append(psum.tile([P, N], F32, name="acc_c%d" % j, tag="bank%d" % (j - EARLY)))
            third(j)
            acc_a = first(j, (1, 0))
            h = h_b[j]
            for acc, col in ((acc_c[j], 1), (acc_a, 2)):
                squares = keep.tile([P, N + 8], F32, name="squares")
                nc.scalar.activation(squares[:, 0:N], acc[:], ACT.Square, scale=ROOT, accum_out=h[:, col : col + 1])
            lowered = keep.tile([P, 3], F32, name="lowered%d" % j)
            low = small("low%d" % j)
            grown = keep.tile([P, 3], F32, name="grown%d" % j)
            summed = small("summed%d" % j)
            inv = small("inv%d" % j)
            w = keep.tile([P, 3], F32, name="w%d" % j)

            def exps():
                nc.vector.tensor_scalar(lowered[:], h[:], -2.0, None, ALU.mult, ALU.min, accum_out=low[:])
                nc.scalar.activation(grown[:], h[:], ACT.Exp, bias=low[:], scale=2.0, accum_out=summed[:])

            steps = [
                exps,
                lambda: nc.vector.reciprocal(inv[:], summed[:]),
                lambda: nc.vector.tensor_scalar(w[:], grown[:], inv[:], None, ALU.mult),
            ]
            return acc_a, w, steps

        def mix_steps(j, acc_a, w):
            total = keep.tile([P, N], F32, name="total%d" % j)
            if j < EARLY:
                addends = [(late[:, j, :], 0), (acc_a[:], 2)]
            else:
                addends = [(acc_b[j][:], 0), (acc_c[j][:], 1), (acc_a[:], 2)]
            steps = []
            for n, (x, col) in enumerate(addends):
                for c0 in (0, half):
                    cols = slice(c0, c0 + half)
                    prior = bias if n == 0 else total
                    steps.append(
                        lambda x=x, col=col, cols=cols, prior=prior: nc.vector.scalar_tensor_tensor(
                            total[:, cols], x[:, cols], w[:, col : col + 1], prior[:, cols], ALU.mult, ALU.add
                        )
                    )
            return total, steps

        for j in range(EARLY):
            pair(j)
        acc_a, w, steps = early_shares(0)
        for step in steps:
            step()
        for j in range(BLOCKS):
            total, wide = mix_steps(j, acc_a, w)
            narrow = []
            if j + 1 < BLOCKS:
                acc_a, w, narrow = early_shares(j + 1) if j + 1 < EARLY else late_shares(j + 1)
            lead = len(wide) - 1 - len(narrow)
            for n, step in enumerate(wide):
                step()
                if lead <= n < lead + len(narrow):
                    narrow[n - lead]()
                if j + 1 == BLOCKS and n >= len(wide) - 2:
                    c0 = (n - len(wide) + 2) * half
                    nc.sync.dma_start(out[j * P : (j + 1) * P, c0 : c0 + half], total[:, c0 : c0 + half])
            if j + 1 < BLOCKS:
                nc.sync.dma_start(out[j * P : (j + 1) * P, :], total[:])
